import numpy as np
import ml_dtypes


def mxq(x, axis, fmt="e4m3"):
    dtype, down = {"e4m3": (ml_dtypes.float8_e4m3fn, 7), "e5m2": (ml_dtypes.float8_e5m2, 14)}[fmt]
    v = np.moveaxis(np.asarray(x, np.float32).astype(ml_dtypes.bfloat16).astype(np.float64), axis, -1)
    blocks = v.reshape(v.shape[:-1] + (-1, 32))
    amax = np.abs(blocks).max(-1, keepdims=True)
    byte = np.maximum(np.where(amax > 0, np.frexp(amax)[1] - 1 + 127, 0) - down, 1)
    scale = np.exp2(byte - 127.0)
    codes = (blocks / scale).astype(np.float32).astype(dtype).astype(np.float64)
    return np.moveaxis((codes * scale).reshape(v.shape), -1, axis)


WIDE = False


def mx_kscale(k):
    if not WIDE:
        return np.ones(k)
    levels = np.array([30, -30])
    if k % 512:
        return np.exp2(np.random.permutation(np.resize(levels, k // 32))).repeat(32)
    a = np.empty((k // 512, 16))
    for p in range(k // 512):
        a[p, :8] = np.random.permutation(np.resize(levels, 8))
        for g in range(8):
            far = levels[np.abs(levels - a[p, g]) >= 10]
            a[p, g + 8] = far[np.random.randint(len(far))]
    return np.exp2(a.ravel()).repeat(32)


def f64(x):
    return np.asarray(x).astype(np.float64)


def striped(idx):
    return np.tile(np.asarray(idx).reshape(-1, 16).T, (8, 1)).astype(np.uint16)


def unstriped(offs):
    return offs[:16].T.reshape(-1).astype(np.int64)


E2M1 = np.array([0.0, 0.5, 1.0, 1.5, 2.0, 3.0, 4.0, 6.0, -0.0, -0.5, -1.0, -1.5, -2.0, -3.0, -4.0, -6.0])


def pack_weight(w, fmt):
    k, n = w.shape
    w = f64(np.asarray(w, np.float32).astype(ml_dtypes.bfloat16)).reshape(k // 32, 32, n)
    amax = np.abs(w).max(1)
    if fmt in ("e4m3", "e5m2"):
        byte = np.frexp(amax)[1] - 1 + 127 - (7 if fmt == "e4m3" else 14)
    else:
        mant, ex = np.frexp(amax / 6.0)
        byte = np.where(mant > 0.5, ex, ex - 1) + 127
    byte = np.clip(np.where(amax > 0, byte, 1), 1, 254)
    scaled = (w * np.exp2(127.0 - byte)[:, None, :]).reshape(k, n).astype(np.float32)
    by_word = np.ascontiguousarray(scaled.reshape(k // 512, 128, 4, n).transpose(0, 1, 3, 2))
    if fmt in ("e4m3", "e5m2"):
        words = by_word.astype(ml_dtypes.float8_e4m3fn if fmt == "e4m3" else ml_dtypes.float8_e5m2).view(np.uint8)
    else:
        c = by_word.astype(ml_dtypes.float4_e2m1fn).view(np.uint8) & 0xF
        words = (c[..., 0::2] | (c[..., 1::2] << 4)).reshape(k // 512, 128, 2 * n)
    return np.ascontiguousarray(words), np.ascontiguousarray(byte.astype(np.uint8).reshape(k // 512, 16, n))


def unpack_weight(words, scales, fmt):
    g, _, n = scales.shape
    words = np.ascontiguousarray(words).reshape(g, 128, n, -1)
    if fmt in ("e4m3", "e5m2"):
        vals = words.view(ml_dtypes.float8_e4m3fn if fmt == "e4m3" else ml_dtypes.float8_e5m2).astype(np.float64)
    else:
        nib = np.empty((g, 128, n, 4), np.uint8)
        nib[..., 0::2] = words & 0xF
        nib[..., 1::2] = words >> 4
        vals = E2M1[nib]
    vals = vals * np.repeat(np.exp2(scales.astype(np.float64) - 127.0), 8, axis=1)[..., None]
    return vals.transpose(0, 1, 3, 2).reshape(g * 512, n)


K, T, J, R, F, Z, O, N, S, E = 512, 1024, 256, 512, 512, 1024, 128, 256, 1024, 512


def setup_inputs():
    n = np.random.standard_normal
    idx = np.random.permutation(T)[:J]
    idx2 = np.random.permutation(Z)[:J]
    idx3 = np.random.permutation(J)[:O]
    idx4 = np.random.permutation(J)[:O]
    idx5 = np.random.permutation(S)[:N]
    idx6 = np.random.permutation(E)[:O]
    idx7 = np.random.permutation(E)[:O]
    fk = mx_kscale(K)
    ff = mx_kscale(F)
    fr = mx_kscale(R)
    xtp = pack_weight(n((K, T)) / fk[:, None], "e2m1")
    xop = pack_weight(n((F, Z)) / ff[:, None], "e4m3")
    wp = pack_weight(n((K, R)) * 1 / np.sqrt(K) * fk[:, None] * fr, "e4m3")
    w0p = pack_weight(n((F, R)) * 1 / np.sqrt(F) * ff[:, None] * fr, "e2m1")
    w2p = pack_weight(n((F, R)) * 1 / np.sqrt(F) * ff[:, None], "e5m2")
    vsp = pack_weight(n((R, S)) * 1 / np.sqrt(R) / fr[:, None], "e2m1")
    return {
        "xt_words": xtp[0],
        "xt_scales": xtp[1],
        "xo_words": xop[0],
        "xo_scales": xop[1],
        "w_words": wp[0],
        "w_scales": wp[1],
        "w0_words": w0p[0],
        "w0_scales": w0p[1],
        "w2_words": w2p[0],
        "w2_scales": w2p[1],
        "vs_words": vsp[0],
        "vs_scales": vsp[1],
        "offs": striped(idx),
        "offs2": striped(idx2),
        "offs3": striped(idx3),
        "offs4": striped(idx4),
        "offs5": striped(idx5),
        "offs6": striped(idx6),
        "offs7": striped(idx7),
    }


def reference(xt_words, xt_scales, xo_words, xo_scales, w_words, w_scales, w0_words, w0_scales, w2_words, w2_scales, vs_words, vs_scales, offs, offs2, offs3, offs4, offs5, offs6, offs7):
    idx = unstriped(offs)
    idx2 = unstriped(offs2)
    idx3 = unstriped(offs3)
    idx4 = unstriped(offs4)
    idx5 = unstriped(offs5)
    idx6 = unstriped(offs6)
    idx7 = unstriped(offs7)
    xtu = unpack_weight(xt_words, xt_scales, "e2m1")
    xou = unpack_weight(xo_words, xo_scales, "e4m3")
    wu = unpack_weight(w_words, w_scales, "e4m3")
    w0u = unpack_weight(w0_words, w0_scales, "e2m1")
    w2u = unpack_weight(w2_words, w2_scales, "e5m2")
    vsu = unpack_weight(vs_words, vs_scales, "e2m1")
    xtidxg = xtu[:, idx]
    xoidx2g = xou[:, idx2]
    a = wu.T @ xtidxg + w0u.T @ xoidx2g
    b = w2u.T @ xoidx2g
    lb = b[:, 0:1]
    la = a[:, 0:1]
    hid = np.abs(a[:, idx3] * lb - b[:, idx4] * la)
    vsidx5g = vsu[:, idx5]
    hidq = mxq(hid, 0, "e5m2")
    p = vsidx5g.T @ hidq
    pa = np.zeros((N, E))
    pa[:, idx6] = p
    pb = np.zeros((N, E))
    pb[:, idx7] = p
    y = pa + pb
    return y

@@ -1,0 +1,173 @@
+from contextlib import ExitStack
+
+import concourse.mybir as mybir
+
+K, T, J, R, F, Z, O, N, S, E = 512, 1024, 256, 512, 512, 1024, 128, 256, 1024, 512
+FLOPS = 2 * (K * R * J + 2 * F * R * J + R * N * O)
+
+F32 = mybir.dt.float32
+BF16 = mybir.dt.bfloat16
+I32 = mybir.dt.int32
+U32 = mybir.dt.uint32
+U16 = mybir.dt.uint16
+U8 = mybir.dt.uint8
+E4M3 = mybir.dt.float8_e4m3fn_x4
+E5M2 = mybir.dt.float8_e5m2_x4
+E2M1 = mybir.dt.float4_e2m1fn_x4
+ACT = mybir.ActivationFunctionType
+ALU = mybir.AluOpType
+
+P = 128
+PACK = 4
+QUADS = 4
+
+
+def tile_list_leadboth_noted_store_pagetwice_kernel(
+    tc, xt_words, xt_scales, xo_words, xo_scales, w_words, w_scales, w0_words, w0_scales,
+    w2_words, w2_scales, vs_words, vs_scales, offs, offs2, offs3, offs4, offs5, offs6, offs7, out,
+):
+    nc = tc.nc
+    with ExitStack() as ctx:
+        sb = ctx.enter_context(tc.tile_pool(name="sb", bufs=1))
+        ps = ctx.enter_context(tc.psum_pool(name="ps", bufs=1))
+
+        def tile(shape, dtype, name, tag=None):
+            return sb.tile(shape, dtype, name=name, tag=tag or name, align_bytes=64)
+
+        def load_list(src, name):
+            lst = tile([P, src.shape[1]], U16, name)
+            nc.sync.dma_start(lst[:], src)
+            return lst
+
+        def load_words(src, cols, dtype, name):
+            words = tile([P, cols], dtype, name)
+            nc.sync.dma_start(words[:].bitcast(I32), src.bitcast(I32))
+            return words
+
+        def zeroed_plane(cols, name):
+            plane = tile([P, cols], U8, name)
+            nc.vector.memset(plane[:].bitcast(I32), 0)
+            return plane
+
+        def load_plane(plane, src, queue):
+            for q in range(QUADS):
+                queue.dma_start(plane[32 * q : 32 * q + 4, :].bitcast(I32), src[0, 4 * q : 4 * q + 4, :].bitcast(I32))
+
+        def gather(window, lst, count, dtype, name, tag=None):
+            got = tile([P, count], dtype, name, tag)
+            nc.vector.tensor_copy(got[:], window[:].indirect(lst[:]))
+            return got
+
+        ws_nat = zeroed_plane(3 * R, "ws_nat")
+        xo_plane = zeroed_plane(Z, "xo_plane")
+        xt_plane = zeroed_plane(T, "xt_plane")
+        vs_plane = zeroed_plane(S, "vs_plane")
+        pages = []
+        for h in range(2):
+            pair = []
+            for side in range(2):
+                page = tile([P, E], F32, "page%d%d" % (h, side))
+                nc.gpsimd.memset(page[:], 0.0)
+                pair.append(page)
+            pages.append(pair)
+
+        ws_stage = tile([4, QUADS, 3, R], U8, "ws_stage")
+        for i, src in enumerate((w2_scales, w_scales, w0_scales)):
+            nc.sync.dma_start(ws_stage[:, :, i, :].bitcast(I32), src[0].rearrange("(q r) c -> r q c", r=4).bitcast(I32))
+        xo_w = load_words(xo_words[0].rearrange("p n t -> p (n t)"), Z, U32, "xo_w")
+        l2 = load_list(offs2, "l2")
+        w2_raw = load_words(w2_words[0].rearrange("p n t -> p (n t)"), R, U32, "w2_raw")
+        w_raw = load_words(w_words[0].rearrange("p n t -> p (n t)"), R, U32, "w_raw")
+        w0_raw = load_words(w0_words[0], R, U16, "w0_raw")
+        load_plane(xo_plane, xo_scales, nc.sync)
+        l1 = load_list(offs, "l1")
+        xt_w = load_words(xt_words[0], T, U16, "xt_w")
+        load_plane(xt_plane, xt_scales, nc.sync)
+        l3 = load_list(offs3, "l3")
+        l4 = load_list(offs4, "l4")
+        l5 = load_list(offs5, "l5")
+        vs_w = load_words(vs_words[0], S, U16, "vs_w")
+        load_plane(vs_plane, vs_scales, nc.sync)
+        l6 = load_list(offs6, "l6")
+        l7 = load_list(offs7, "l7")
+
+        for q in range(QUADS):
+            nc.vector.tensor_copy(
+                ws_nat[32 * q : 32 * q + 4, :].bitcast(I32),
+                ws_stage[:, q, :, :].rearrange("r i c -> r (i c)").bitcast(I32),
+            )
+        ws = tile([P, 3, PACK, P], U8, "ws")
+        nc.vector.tensor_copy(
+            ws[:].rearrange("p i t m -> p t i m"),
+            ws_nat[:].rearrange("p (i m t) -> p t i m", i=3, t=PACK),
+        )
+        xo_gw = gather(xo_w, l2, J, U32, "xo_gw")
+        xo_gs = gather(xo_plane, l2, J, U8, "xo_gs")
+        xt_gw = gather(xt_w, l1, J, U16, "xt_gw")
+        xt_gs = gather(xt_plane, l1, J, U8, "xt_gs")
+
+        def deal(raw, dtype, name):
+            dealt = tile([P, PACK, P], dtype, name)
+            nc.scalar.copy(dealt[:].rearrange("p t m -> p m t"), raw[:].rearrange("p (m t) -> p m t", t=PACK))
+            return dealt
+
+        w2_d = deal(w2_raw, U32, "w2_d")
+        w_d = deal(w_raw, U32, "w_d")
+        w0_d = deal(w0_raw, U16, "w0_d")
+
+        b_sb = []
+        for t in range(PACK):
+            b_ps = ps.tile([P, J], F32, name="b_ps%d" % t, tag="bank%d" % t)
+            nc.tensor.matmul_mx(b_ps[:], lhsT=w2_d[:, t, :].bitcast(E5M2), lhsT_scale=ws[:, 0, t, :],
+                                rhs=xo_gw[:].bitcast(E4M3), rhs_scale=xo_gs[:], start=True, stop=True)
+            rows = tile([P, J], F32, "b_sb%d" % t)
+            nc.scalar.copy(rows[:], b_ps[:])
+            b_sb.append(rows)
+
+        diff = tile([P, PACK, O], F32, "diff")
+        ga = [tile([P, PACK - 1, O], F32, "ga_first"), tile([P, 1, O], F32, "ga_last")]
+        gb = [tile([P, PACK - 1, O], F32, "gb_first"), tile([P, 1, O], F32, "gb_last")]
+        for t in range(PACK):
+            a_ps = ps.tile([P, J], F32, name="a_ps%d" % t, tag="bank%d" % (PACK + t))
+            nc.tensor.matmul_mx(a_ps[:], lhsT=w_d[:, t, :].bitcast(E4M3), lhsT_scale=ws[:, 1, t, :],
+                                rhs=xt_gw[:].bitcast(E2M1), rhs_scale=xt_gs[:], start=True, stop=False)
+            nc.tensor.matmul_mx(a_ps[:], lhsT=w0_d[:, t, :].bitcast(E2M1), lhsT_scale=ws[:, 2, t, :],
+                                rhs=xo_gw[:].bitcast(E4M3), rhs_scale=xo_gs[:], start=False, stop=True)
+            a_sb = tile([P, J], F32, "a_sb%d" % t)
+            nc.vector.tensor_copy(a_sb[:], a_ps[:])
+            part, place = divmod(t, PACK - 1)
+            nc.scalar.activation(out=ga[part][:, place, :], in_=a_sb[:].indirect(l3[:]), func=ACT.Copy, scale=b_sb[t][:, 0:1])
+            nc.scalar.activation(out=gb[part][:, place, :], in_=b_sb[t][:].indirect(l4[:]), func=ACT.Copy, scale=a_sb[:, 0:1])
+
+        vs_gw = gather(vs_w, l5, N, U16, "vs_gw", "xo_gw")
+        nc.vector.tensor_tensor(diff[:, 0 : PACK - 1, :], ga[0][:], gb[0][:], ALU.subtract)
+        nc.vector.tensor_tensor(diff[:, PACK - 1 : PACK, :], ga[1][:], gb[1][:], ALU.subtract)
+        vs_gs = gather(vs_plane, l5, N, U8, "vs_gs", "ga_last")
+        hid = tile([P, O, PACK], BF16, "hid")
+        nc.scalar.activation(out=hid[:], in_=diff[:].rearrange("p t o -> p o t"), func=ACT.Abs)
+        hid_w = tile([P, O], U32, "hid_w")
+        hid_s = tile([P, O], U8, "hid_s")
+        nc.vector.quantize_mx(hid_w[:].bitcast(E5M2), hid_s[:], hid[:].rearrange("p o t -> p (o t)"))
+
+        prods = []
+        for h in range(2):
+            p_ps = ps.tile([P, O], F32, name="p_ps%d" % h, tag="bank%d" % h)
+            nc.tensor.matmul_mx(p_ps[:], lhsT=vs_gw[:, h * P : (h + 1) * P].bitcast(E2M1), lhsT_scale=vs_gs[:, h * P : (h + 1) * P],
+                                rhs=hid_w[:].bitcast(E5M2), rhs_scale=hid_s[:], start=True, stop=True)
+            p_sb = tile([P, O], F32, "p_sb%d" % h)
+            if h == 0:
+                nc.scalar.copy(p_sb[:], p_ps[:])
+            else:
+                nc.vector.tensor_copy(p_sb[:], p_ps[:])
+            prods.append(p_sb)
+
+        for h in range(2):
+            pa, pb = pages[h]
+            nc.scalar.activation(out=pa[:].indirect(l6[:]), in_=prods[h][:], func=ACT.Copy)
+            nc.vector.tensor_copy(pb[:].indirect(l7[:]), prods[h][:])
+            pieces = 1 + h
+            for c in range(pieces):
+                cols = slice(c * E // pieces, (c + 1) * E // pieces)
+                res = tile([P, E // pieces], F32, "res%d%d" % (h, c))
+                nc.vector.tensor_tensor(res[:], pa[:, cols], pb[:, cols], ALU.add)
+                nc.sync.dma_start(out[h * P : (h + 1) * P, cols], res[:])

@@ -20,6 +20,7 @@ ALU = mybir.AluOpType
 P = 128
 PACK = 4
 QUADS = 4
+ABS_SPLIT = 80
 
 
 def tile_list_leadboth_noted_store_pagetwice_kernel(
@@ -44,13 +45,13 @@ def tile_list_leadboth_noted_store_pagetwice_kernel(
             nc.sync.dma_start(words[:].bitcast(I32), src.bitcast(I32))
             return words
 
-        def zeroed_plane(cols, name):
+        def zeroed_plane(cols, name, engine):
             plane = tile([P, cols], U8, name)
-            nc.vector.memset(plane[:].bitcast(I32), 0)
+            engine.memset(plane[:].bitcast(I32), 0)
             return plane
 
-        def load_plane(plane, src, queue):
-            for q in range(QUADS):
+        def load_plane(plane, src, queue, quads=range(QUADS)):
+            for q in quads:
                 queue.dma_start(plane[32 * q : 32 * q + 4, :].bitcast(I32), src[0, 4 * q : 4 * q + 4, :].bitcast(I32))
 
         def gather(window, lst, count, dtype, name, tag=None):
@@ -58,30 +59,22 @@ def tile_list_leadboth_noted_store_pagetwice_kernel(
             nc.vector.tensor_copy(got[:], window[:].indirect(lst[:]))
             return got
 
-        ws_nat = zeroed_plane(3 * R, "ws_nat")
-        xo_plane = zeroed_plane(Z, "xo_plane")
-        xt_plane = zeroed_plane(T, "xt_plane")
-        vs_plane = zeroed_plane(S, "vs_plane")
-        pages = []
-        for h in range(2):
-            pair = []
-            for side in range(2):
-                page = tile([P, E], F32, "page%d%d" % (h, side))
-                nc.gpsimd.memset(page[:], 0.0)
-                pair.append(page)
-            pages.append(pair)
+        xo_plane = zeroed_plane(Z, "xo_plane", nc.vector)
+        xt_plane = zeroed_plane(T, "xt_plane", nc.vector)
+        ws_nat = zeroed_plane(3 * R, "ws_nat", nc.vector)
+        vs_plane = zeroed_plane(S, "vs_plane", nc.vector)
 
         ws_stage = tile([4, QUADS, 3, R], U8, "ws_stage")
-        for i, src in enumerate((w2_scales, w_scales, w0_scales)):
+        for i, src in enumerate((w2_scales, w0_scales, w_scales)):
             nc.sync.dma_start(ws_stage[:, :, i, :].bitcast(I32), src[0].rearrange("(q r) c -> r q c", r=4).bitcast(I32))
-        xo_w = load_words(xo_words[0].rearrange("p n t -> p (n t)"), Z, U32, "xo_w")
         l2 = load_list(offs2, "l2")
-        w2_raw = load_words(w2_words[0].rearrange("p n t -> p (n t)"), R, U32, "w2_raw")
-        w_raw = load_words(w_words[0].rearrange("p n t -> p (n t)"), R, U32, "w_raw")
-        w0_raw = load_words(w0_words[0], R, U16, "w0_raw")
-        load_plane(xo_plane, xo_scales, nc.sync)
         l1 = load_list(offs, "l1")
+        xo_w = load_words(xo_words[0].rearrange("p n t -> p (n t)"), Z, U32, "xo_w")
         xt_w = load_words(xt_words[0], T, U16, "xt_w")
+        load_plane(xo_plane, xo_scales, nc.sync)
+        w2_raw = load_words(w2_words[0].rearrange("p n t -> p (n t)"), R, U32, "w2_raw")
+        w0_raw = load_words(w0_words[0], R, U16, "w0_raw")
+        w_raw = load_words(w_words[0].rearrange("p n t -> p (n t)"), R, U32, "w_raw")
         load_plane(xt_plane, xt_scales, nc.sync)
         l3 = load_list(offs3, "l3")
         l4 = load_list(offs4, "l4")
@@ -96,29 +89,41 @@ def tile_list_leadboth_noted_store_pagetwice_kernel(
                 ws_nat[32 * q : 32 * q + 4, :].bitcast(I32),
                 ws_stage[:, q, :, :].rearrange("r i c -> r (i c)").bitcast(I32),
             )
-        ws = tile([P, 3, PACK, P], U8, "ws")
-        nc.vector.tensor_copy(
-            ws[:].rearrange("p i t m -> p t i m"),
-            ws_nat[:].rearrange("p (i m t) -> p t i m", i=3, t=PACK),
-        )
+        ws_by_t = ws_nat[:].rearrange("p (i m t) -> p t i m", i=3, t=PACK)
+        w2_s = tile([P, PACK, P], U8, "w2_s")
+        nc.vector.tensor_copy(w2_s[:], ws_by_t[:, :, 0, :])
+        a_s_first = tile([P, 1, 2, P], U8, "a_s_first")
+        nc.vector.tensor_copy(a_s_first[:], ws_by_t[:, 0:1, 1:3, :])
         xo_gw = gather(xo_w, l2, J, U32, "xo_gw")
         xo_gs = gather(xo_plane, l2, J, U8, "xo_gs")
         xt_gw = gather(xt_w, l1, J, U16, "xt_gw")
         xt_gs = gather(xt_plane, l1, J, U8, "xt_gs")
+        a_s_rest = tile([P, PACK - 1, 2, P], U8, "a_s_rest", "xt_plane")
+        nc.vector.tensor_copy(a_s_rest[:].rearrange("p t i m -> p i t m"), ws_by_t[:, 1:PACK, 1:3, :].rearrange("p t i m -> p i t m"))
+        a_s = [a_s_first[:, 0]] + [a_s_rest[:, t] for t in range(PACK - 1)]
 
-        def deal(raw, dtype, name):
+        def deal(raw, dtype, name, walk):
             dealt = tile([P, PACK, P], dtype, name)
-            nc.scalar.copy(dealt[:].rearrange("p t m -> p m t"), raw[:].rearrange("p (m t) -> p m t", t=PACK))
+            nc.scalar.copy(dealt[:].rearrange("p t m -> " + walk), raw[:].rearrange("p (m t) -> " + walk, t=PACK))
             return dealt
 
-        w2_d = deal(w2_raw, U32, "w2_d")
-        w_d = deal(w_raw, U32, "w_d")
-        w0_d = deal(w0_raw, U16, "w0_d")
+        w2_d = deal(w2_raw, U32, "w2_d", "p m t")
+        w0_d = deal(w0_raw, U16, "w0_d", "p t m")
+        w_d = deal(w_raw, U32, "w_d", "p m t")
+
+        pages = []
+        for h, tags in enumerate((("w2_raw", "w_raw"), ("xo_w", "xt_w"))):
+            pair = []
+            for side in range(2):
+                page = tile([P, E], F32, "page%d%d" % (h, side), tags[side])
+                nc.gpsimd.memset(page[:], 0.0)
+                pair.append(page)
+            pages.append(pair)
 
         b_sb = []
         for t in range(PACK):
             b_ps = ps.tile([P, J], F32, name="b_ps%d" % t, tag="bank%d" % t)
-            nc.tensor.matmul_mx(b_ps[:], lhsT=w2_d[:, t, :].bitcast(E5M2), lhsT_scale=ws[:, 0, t, :],
+            nc.tensor.matmul_mx(b_ps[:], lhsT=w2_d[:, t, :].bitcast(E5M2), lhsT_scale=w2_s[:, t, :],
                                 rhs=xo_gw[:].bitcast(E4M3), rhs_scale=xo_gs[:], start=True, stop=True)
             rows = tile([P, J], F32, "b_sb%d" % t)
             nc.scalar.copy(rows[:], b_ps[:])
@@ -129,22 +134,25 @@ def tile_list_leadboth_noted_store_pagetwice_kernel(
         gb = [tile([P, PACK - 1, O], F32, "gb_first"), tile([P, 1, O], F32, "gb_last")]
         for t in range(PACK):
             a_ps = ps.tile([P, J], F32, name="a_ps%d" % t, tag="bank%d" % (PACK + t))
-            nc.tensor.matmul_mx(a_ps[:], lhsT=w_d[:, t, :].bitcast(E4M3), lhsT_scale=ws[:, 1, t, :],
-                                rhs=xt_gw[:].bitcast(E2M1), rhs_scale=xt_gs[:], start=True, stop=False)
-            nc.tensor.matmul_mx(a_ps[:], lhsT=w0_d[:, t, :].bitcast(E2M1), lhsT_scale=ws[:, 2, t, :],
-                                rhs=xo_gw[:].bitcast(E4M3), rhs_scale=xo_gs[:], start=False, stop=True)
+            nc.tensor.matmul_mx(a_ps[:], lhsT=w0_d[:, t, :].bitcast(E2M1), lhsT_scale=a_s[t][:, 0, :],
+                                rhs=xo_gw[:].bitcast(E4M3), rhs_scale=xo_gs[:], start=True, stop=False)
+            nc.tensor.matmul_mx(a_ps[:], lhsT=w_d[:, t, :].bitcast(E4M3), lhsT_scale=a_s[t][:, 1, :],
+                                rhs=xt_gw[:].bitcast(E2M1), rhs_scale=xt_gs[:], start=False, stop=True)
             a_sb = tile([P, J], F32, "a_sb%d" % t)
             nc.vector.tensor_copy(a_sb[:], a_ps[:])
             part, place = divmod(t, PACK - 1)
             nc.scalar.activation(out=ga[part][:, place, :], in_=a_sb[:].indirect(l3[:]), func=ACT.Copy, scale=b_sb[t][:, 0:1])
             nc.scalar.activation(out=gb[part][:, place, :], in_=b_sb[t][:].indirect(l4[:]), func=ACT.Copy, scale=a_sb[:, 0:1])
 
-        vs_gw = gather(vs_w, l5, N, U16, "vs_gw", "xo_gw")
+        vs_gw = gather(vs_w, l5, N, U16, "vs_gw", "xt_gw")
+        vs_gs = gather(vs_plane, l5, N, U8, "vs_gs", "xt_gs")
         nc.vector.tensor_tensor(diff[:, 0 : PACK - 1, :], ga[0][:], gb[0][:], ALU.subtract)
         nc.vector.tensor_tensor(diff[:, PACK - 1 : PACK, :], ga[1][:], gb[1][:], ALU.subtract)
-        vs_gs = gather(vs_plane, l5, N, U8, "vs_gs", "ga_last")
+
         hid = tile([P, O, PACK], BF16, "hid")
-        nc.scalar.activation(out=hid[:], in_=diff[:].rearrange("p t o -> p o t"), func=ACT.Abs)
+        diff_by_o = diff[:].rearrange("p t o -> p o t")
+        nc.scalar.activation(out=hid[:, 0:ABS_SPLIT, :], in_=diff_by_o[:, 0:ABS_SPLIT, :], func=ACT.Abs)
+        nc.vector.scalar_tensor_tensor(hid[:, ABS_SPLIT:O, :], diff_by_o[:, ABS_SPLIT:O, :], -1.0, diff_by_o[:, ABS_SPLIT:O, :], ALU.mult, ALU.max)
         hid_w = tile([P, O], U32, "hid_w")
         hid_s = tile([P, O], U8, "hid_s")
         nc.vector.quantize_mx(hid_w[:].bitcast(E5M2), hid_s[:], hid[:].rearrange("p o t -> p (o t)"))
@@ -161,13 +169,16 @@ def tile_list_leadboth_noted_store_pagetwice_kernel(
                 nc.vector.tensor_copy(p_sb[:], p_ps[:])
             prods.append(p_sb)
 
-        for h in range(2):
+        def add_and_store(h, pieces):
             pa, pb = pages[h]
-            nc.scalar.activation(out=pa[:].indirect(l6[:]), in_=prods[h][:], func=ACT.Copy)
-            nc.vector.tensor_copy(pb[:].indirect(l7[:]), prods[h][:])
-            pieces = 1 + h
             for c in range(pieces):
                 cols = slice(c * E // pieces, (c + 1) * E // pieces)
                 res = tile([P, E // pieces], F32, "res%d%d" % (h, c))
                 nc.vector.tensor_tensor(res[:], pa[:, cols], pb[:, cols], ALU.add)
                 nc.sync.dma_start(out[h * P : (h + 1) * P, cols], res[:])
+
+        for h in range(2):
+            nc.scalar.activation(out=pages[h][0][:].indirect(l6[:]), in_=prods[h][:], func=ACT.Copy)
+            nc.vector.tensor_copy(pages[h][1][:].indirect(l7[:]), prods[h][:])
+        add_and_store(0, 2)
+        add_and_store(1, 2)

@@ -59,10 +59,22 @@ def tile_list_leadboth_noted_store_pagetwice_kernel(
             nc.vector.tensor_copy(got[:], window[:].indirect(lst[:]))
             return got
 
-        xo_plane = zeroed_plane(Z, "xo_plane", nc.vector)
-        xt_plane = zeroed_plane(T, "xt_plane", nc.vector)
+        xo_plane = zeroed_plane(Z, "xo_plane", nc.gpsimd)
+        load_plane(xo_plane, xo_scales, nc.gpsimd, range(0, 1))
+        xt_plane = zeroed_plane(T, "xt_plane", nc.gpsimd)
+        load_plane(xt_plane, xt_scales, nc.gpsimd, range(0, 1))
         ws_nat = zeroed_plane(3 * R, "ws_nat", nc.vector)
         vs_plane = zeroed_plane(S, "vs_plane", nc.vector)
+
+        def zeroed_pages(h, engine, tags):
+            pair = []
+            for side in range(2):
+                page = tile([P, E], F32, "page%d%d" % (h, side), tags[side])
+                engine.memset(page[:], 0.0)
+                pair.append(page)
+            return pair
+
+        pages = [zeroed_pages(0, nc.vector, (None, None))]
 
         ws_stage = tile([4, QUADS, 3, R], U8, "ws_stage")
         for i, src in enumerate((w2_scales, w0_scales, w_scales)):
@@ -70,12 +82,12 @@ def tile_list_leadboth_noted_store_pagetwice_kernel(
         l2 = load_list(offs2, "l2")
         l1 = load_list(offs, "l1")
         xo_w = load_words(xo_words[0].rearrange("p n t -> p (n t)"), Z, U32, "xo_w")
-        xt_w = load_words(xt_words[0], T, U16, "xt_w")
-        load_plane(xo_plane, xo_scales, nc.sync)
         w2_raw = load_words(w2_words[0].rearrange("p n t -> p (n t)"), R, U32, "w2_raw")
         w0_raw = load_words(w0_words[0], R, U16, "w0_raw")
+        load_plane(xo_plane, xo_scales, nc.sync, range(1, 4))
         w_raw = load_words(w_words[0].rearrange("p n t -> p (n t)"), R, U32, "w_raw")
-        load_plane(xt_plane, xt_scales, nc.sync)
+        xt_w = load_words(xt_words[0], T, U16, "xt_w")
+        load_plane(xt_plane, xt_scales, nc.sync, range(1, 4))
         l3 = load_list(offs3, "l3")
         l4 = load_list(offs4, "l4")
         l5 = load_list(offs5, "l5")
@@ -91,16 +103,16 @@ def tile_list_leadboth_noted_store_pagetwice_kernel(
             )
         ws_by_t = ws_nat[:].rearrange("p (i m t) -> p t i m", i=3, t=PACK)
         w2_s = tile([P, PACK, P], U8, "w2_s")
-        nc.vector.tensor_copy(w2_s[:], ws_by_t[:, :, 0, :])
-        a_s_first = tile([P, 1, 2, P], U8, "a_s_first")
-        nc.vector.tensor_copy(a_s_first[:], ws_by_t[:, 0:1, 1:3, :])
+        nc.gpsimd.tensor_copy(w2_s[:], ws_by_t[:, :, 0, :])
+        a_s_early = tile([P, 2, 2, P], U8, "a_s_early")
+        nc.gpsimd.tensor_copy(a_s_early[:], ws_by_t[:, 0:2, 1:3, :])
         xo_gw = gather(xo_w, l2, J, U32, "xo_gw")
         xo_gs = gather(xo_plane, l2, J, U8, "xo_gs")
         xt_gw = gather(xt_w, l1, J, U16, "xt_gw")
         xt_gs = gather(xt_plane, l1, J, U8, "xt_gs")
-        a_s_rest = tile([P, PACK - 1, 2, P], U8, "a_s_rest", "xt_plane")
-        nc.vector.tensor_copy(a_s_rest[:].rearrange("p t i m -> p i t m"), ws_by_t[:, 1:PACK, 1:3, :].rearrange("p t i m -> p i t m"))
-        a_s = [a_s_first[:, 0]] + [a_s_rest[:, t] for t in range(PACK - 1)]
+        a_s_late = tile([P, 2, 2, P], U8, "a_s_late", "xt_plane")
+        nc.vector.tensor_copy(a_s_late[:], ws_by_t[:, 2:4, 1:3, :])
+        a_s = [a_s_early[:, 0], a_s_early[:, 1], a_s_late[:, 0], a_s_late[:, 1]]
 
         def deal(raw, dtype, name, walk):
             dealt = tile([P, PACK, P], dtype, name)
@@ -111,15 +123,8 @@ def tile_list_leadboth_noted_store_pagetwice_kernel(
         w0_d = deal(w0_raw, U16, "w0_d", "p t m")
         w_d = deal(w_raw, U32, "w_d", "p m t")
 
-        pages = []
-        for h, tags in enumerate((("w2_raw", "w_raw"), ("xo_w", "xt_w"))):
-            pair = []
-            for side in range(2):
-                page = tile([P, E], F32, "page%d%d" % (h, side), tags[side])
-                nc.gpsimd.memset(page[:], 0.0)
-                pair.append(page)
-            pages.append(pair)
 
+        pages.append(zeroed_pages(1, nc.gpsimd, ("xo_w", "w2_raw")))
         b_sb = []
         for t in range(PACK):
             b_ps = ps.tile([P, J], F32, name="b_ps%d" % t, tag="bank%d" % t)
@@ -129,7 +134,6 @@ def tile_list_leadboth_noted_store_pagetwice_kernel(
             nc.scalar.copy(rows[:], b_ps[:])
             b_sb.append(rows)
 
-        diff = tile([P, PACK, O], F32, "diff")
         ga = [tile([P, PACK - 1, O], F32, "ga_first"), tile([P, 1, O], F32, "ga_last")]
         gb = [tile([P, PACK - 1, O], F32, "gb_first"), tile([P, 1, O], F32, "gb_last")]
         for t in range(PACK):
@@ -145,7 +149,8 @@ def tile_list_leadboth_noted_store_pagetwice_kernel(
             nc.scalar.activation(out=gb[part][:, place, :], in_=b_sb[t][:].indirect(l4[:]), func=ACT.Copy, scale=a_sb[:, 0:1])
 
         vs_gw = gather(vs_w, l5, N, U16, "vs_gw", "xt_gw")
-        vs_gs = gather(vs_plane, l5, N, U8, "vs_gs", "xt_gs")
+        vs_gs = gather(vs_plane, l5, N, U8, "vs_gs", "vs_w")
+        diff = tile([P, PACK, O], F32, "diff", "vs_plane")
         nc.vector.tensor_tensor(diff[:, 0 : PACK - 1, :], ga[0][:], gb[0][:], ALU.subtract)
         nc.vector.tensor_tensor(diff[:, PACK - 1 : PACK, :], ga[1][:], gb[1][:], ALU.subtract)
 

from contextlib import ExitStack

import concourse.mybir as mybir

K, T, J, R, F, Z, O, N, S, E = 512, 1024, 256, 512, 512, 1024, 128, 256, 1024, 512
FLOPS = 2 * (K * R * J + 2 * F * R * J + R * N * O)

F32 = mybir.dt.float32
BF16 = mybir.dt.bfloat16
I32 = mybir.dt.int32
U32 = mybir.dt.uint32
U16 = mybir.dt.uint16
U8 = mybir.dt.uint8
E4M3 = mybir.dt.float8_e4m3fn_x4
E5M2 = mybir.dt.float8_e5m2_x4
E2M1 = mybir.dt.float4_e2m1fn_x4
ACT = mybir.ActivationFunctionType
ALU = mybir.AluOpType

P = 128
PACK = 4
QUADS = 4
ABS_SPLIT = 80


def tile_list_leadboth_noted_store_pagetwice_kernel(
    tc, xt_words, xt_scales, xo_words, xo_scales, w_words, w_scales, w0_words, w0_scales,
    w2_words, w2_scales, vs_words, vs_scales, offs, offs2, offs3, offs4, offs5, offs6, offs7, out,
):
    nc = tc.nc
    with ExitStack() as ctx:
        sb = ctx.enter_context(tc.tile_pool(name="sb", bufs=1))
        ps = ctx.enter_context(tc.psum_pool(name="ps", bufs=1))

        def tile(shape, dtype, name, tag=None):
            return sb.tile(shape, dtype, name=name, tag=tag or name, align_bytes=64)

        def load_list(src, name):
            lst = tile([P, src.shape[1]], U16, name)
            nc.sync.dma_start(lst[:], src)
            return lst

        def load_words(src, cols, dtype, name):
            words = tile([P, cols], dtype, name)
            nc.sync.dma_start(words[:].bitcast(I32), src.bitcast(I32))
            return words

        def zeroed_plane(cols, name, engine):
            plane = tile([P, cols], U8, name)
            engine.memset(plane[:].bitcast(I32), 0)
            return plane

        def load_plane(plane, src, queue, quads=range(QUADS)):
            for q in quads:
                queue.dma_start(plane[32 * q : 32 * q + 4, :].bitcast(I32), src[0, 4 * q : 4 * q + 4, :].bitcast(I32))

        def gather(window, lst, count, dtype, name, tag=None):
            got = tile([P, count], dtype, name, tag)
            nc.vector.tensor_copy(got[:], window[:].indirect(lst[:]))
            return got

        xo_plane = zeroed_plane(Z, "xo_plane", nc.gpsimd)
        load_plane(xo_plane, xo_scales, nc.gpsimd, range(0, 1))
        xt_plane = zeroed_plane(T, "xt_plane", nc.gpsimd)
        load_plane(xt_plane, xt_scales, nc.gpsimd, range(0, 1))
        ws_nat = zeroed_plane(3 * R, "ws_nat", nc.vector)
        vs_plane = zeroed_plane(S, "vs_plane", nc.vector)

        def zeroed_pages(h, engine, tags):
            pair = []
            for side in range(2):
                page = tile([P, E], F32, "page%d%d" % (h, side), tags[side])
                engine.memset(page[:], 0.0)
                pair.append(page)
            return pair

        pages = [zeroed_pages(0, nc.vector, (None, None))]

        ws_stage = tile([4, QUADS, 3, R], U8, "ws_stage")
        for i, src in enumerate((w2_scales, w0_scales, w_scales)):
            nc.sync.dma_start(ws_stage[:, :, i, :].bitcast(I32), src[0].rearrange("(q r) c -> r q c", r=4).bitcast(I32))
        l2 = load_list(offs2, "l2")
        l1 = load_list(offs, "l1")
        xo_w = load_words(xo_words[0].rearrange("p n t -> p (n t)"), Z, U32, "xo_w")
        w2_raw = load_words(w2_words[0].rearrange("p n t -> p (n t)"), R, U32, "w2_raw")
        w0_raw = load_words(w0_words[0], R, U16, "w0_raw")
        load_plane(xo_plane, xo_scales, nc.sync, range(1, 4))
        w_raw = load_words(w_words[0].rearrange("p n t -> p (n t)"), R, U32, "w_raw")
        xt_w = load_words(xt_words[0], T, U16, "xt_w")
        load_plane(xt_plane, xt_scales, nc.sync, range(1, 4))
        l3 = load_list(offs3, "l3")
        l4 = load_list(offs4, "l4")
        l5 = load_list(offs5, "l5")
        vs_w = load_words(vs_words[0], S, U16, "vs_w")
        load_plane(vs_plane, vs_scales, nc.sync)
        l6 = load_list(offs6, "l6")
        l7 = load_list(offs7, "l7")

        for q in range(QUADS):
            nc.vector.tensor_copy(
                ws_nat[32 * q : 32 * q + 4, :].bitcast(I32),
                ws_stage[:, q, :, :].rearrange("r i c -> r (i c)").bitcast(I32),
            )
        ws_by_t = ws_nat[:].rearrange("p (i m t) -> p t i m", i=3, t=PACK)
        w2_s = tile([P, PACK, P], U8, "w2_s")
        nc.gpsimd.tensor_copy(w2_s[:], ws_by_t[:, :, 0, :])
        a_s_early = tile([P, 2, 2, P], U8, "a_s_early")
        nc.gpsimd.tensor_copy(a_s_early[:], ws_by_t[:, 0:2, 1:3, :])
        xo_gw = gather(xo_w, l2, J, U32, "xo_gw")
        xo_gs = gather(xo_plane, l2, J, U8, "xo_gs")
        xt_gw = gather(xt_w, l1, J, U16, "xt_gw")
        xt_gs = gather(xt_plane, l1, J, U8, "xt_gs")
        a_s_late = tile([P, 2, 2, P], U8, "a_s_late", "xt_plane")
        nc.vector.tensor_copy(a_s_late[:], ws_by_t[:, 2:4, 1:3, :])
        a_s = [a_s_early[:, 0], a_s_early[:, 1], a_s_late[:, 0], a_s_late[:, 1]]

        def deal(raw, dtype, name, walk):
            dealt = tile([P, PACK, P], dtype, name)
            nc.scalar.copy(dealt[:].rearrange("p t m -> " + walk), raw[:].rearrange("p (m t) -> " + walk, t=PACK))
            return dealt

        w2_d = deal(w2_raw, U32, "w2_d", "p m t")
        w0_d = deal(w0_raw, U16, "w0_d", "p t m")
        w_d = deal(w_raw, U32, "w_d", "p m t")


        pages.append(zeroed_pages(1, nc.gpsimd, ("xo_w", "w2_raw")))
        b_sb = []
        for t in range(PACK):
            b_ps = ps.tile([P, J], F32, name="b_ps%d" % t, tag="bank%d" % t)
            nc.tensor.matmul_mx(b_ps[:], lhsT=w2_d[:, t, :].bitcast(E5M2), lhsT_scale=w2_s[:, t, :],
                                rhs=xo_gw[:].bitcast(E4M3), rhs_scale=xo_gs[:], start=True, stop=True)
            rows = tile([P, J], F32, "b_sb%d" % t)
            nc.scalar.copy(rows[:], b_ps[:])
            b_sb.append(rows)

        ga = [tile([P, PACK - 1, O], F32, "ga_first"), tile([P, 1, O], F32, "ga_last")]
        gb = [tile([P, PACK - 1, O], F32, "gb_first"), tile([P, 1, O], F32, "gb_last")]
        for t in range(PACK):
            a_ps = ps.tile([P, J], F32, name="a_ps%d" % t, tag="bank%d" % (PACK + t))
            nc.tensor.matmul_mx(a_ps[:], lhsT=w0_d[:, t, :].bitcast(E2M1), lhsT_scale=a_s[t][:, 0, :],
                                rhs=xo_gw[:].bitcast(E4M3), rhs_scale=xo_gs[:], start=True, stop=False)
            nc.tensor.matmul_mx(a_ps[:], lhsT=w_d[:, t, :].bitcast(E4M3), lhsT_scale=a_s[t][:, 1, :],
                                rhs=xt_gw[:].bitcast(E2M1), rhs_scale=xt_gs[:], start=False, stop=True)
            a_sb = tile([P, J], F32, "a_sb%d" % t)
            nc.vector.tensor_copy(a_sb[:], a_ps[:])
            part, place = divmod(t, PACK - 1)
            nc.scalar.activation(out=ga[part][:, place, :], in_=a_sb[:].indirect(l3[:]), func=ACT.Copy, scale=b_sb[t][:, 0:1])
            nc.scalar.activation(out=gb[part][:, place, :], in_=b_sb[t][:].indirect(l4[:]), func=ACT.Copy, scale=a_sb[:, 0:1])

        vs_gw = gather(vs_w, l5, N, U16, "vs_gw", "xt_gw")
        vs_gs = gather(vs_plane, l5, N, U8, "vs_gs", "vs_w")
        diff = tile([P, PACK, O], F32, "diff", "vs_plane")
        nc.vector.tensor_tensor(diff[:, 0 : PACK - 1, :], ga[0][:], gb[0][:], ALU.subtract)
        nc.vector.tensor_tensor(diff[:, PACK - 1 : PACK, :], ga[1][:], gb[1][:], ALU.subtract)

        hid = tile([P, O, PACK], BF16, "hid")
        diff_by_o = diff[:].rearrange("p t o -> p o t")
        nc.scalar.activation(out=hid[:, 0:ABS_SPLIT, :], in_=diff_by_o[:, 0:ABS_SPLIT, :], func=ACT.Abs)
        nc.vector.scalar_tensor_tensor(hid[:, ABS_SPLIT:O, :], diff_by_o[:, ABS_SPLIT:O, :], -1.0, diff_by_o[:, ABS_SPLIT:O, :], ALU.mult, ALU.max)
        hid_w = tile([P, O], U32, "hid_w")
        hid_s = tile([P, O], U8, "hid_s")
        nc.vector.quantize_mx(hid_w[:].bitcast(E5M2), hid_s[:], hid[:].rearrange("p o t -> p (o t)"))

        prods = []
        for h in range(2):
            p_ps = ps.tile([P, O], F32, name="p_ps%d" % h, tag="bank%d" % h)
            nc.tensor.matmul_mx(p_ps[:], lhsT=vs_gw[:, h * P : (h + 1) * P].bitcast(E2M1), lhsT_scale=vs_gs[:, h * P : (h + 1) * P],
                                rhs=hid_w[:].bitcast(E5M2), rhs_scale=hid_s[:], start=True, stop=True)
            p_sb = tile([P, O], F32, "p_sb%d" % h)
            if h == 0:
                nc.scalar.copy(p_sb[:], p_ps[:])
            else:
                nc.vector.tensor_copy(p_sb[:], p_ps[:])
            prods.append(p_sb)

        def add_and_store(h, pieces):
            pa, pb = pages[h]
            for c in range(pieces):
                cols = slice(c * E // pieces, (c + 1) * E // pieces)
                res = tile([P, E // pieces], F32, "res%d%d" % (h, c))
                nc.vector.tensor_tensor(res[:], pa[:, cols], pb[:, cols], ALU.add)
                nc.sync.dma_start(out[h * P : (h + 1) * P, cols], res[:])

        for h in range(2):
            nc.scalar.activation(out=pages[h][0][:].indirect(l6[:]), in_=prods[h][:], func=ACT.Copy)
            nc.vector.tensor_copy(pages[h][1][:].indirect(l7[:]), prods[h][:])
        add_and_store(0, 2)
        add_and_store(1, 2)
